import numpy as np, ml_dtypes
CORES = [5,29,101,125,133,157,229,253]
N = 8
import mx_ref
BF = ml_dtypes.bfloat16
def f(rng, *shape):
    return mx_ref.flush((rng.standard_normal(shape, dtype=np.float32) * np.exp2(rng.integers(-2, 3, shape[:-1] + (1,)))).astype(BF))
def wide(rng, *shape, cols=0):
    v = rng.standard_normal(shape, dtype=np.float32) * np.exp2(rng.integers(-12, 13, shape)).astype(np.float32)
    if cols: v *= np.repeat(np.exp2(rng.integers(-cols, cols + 1, shape[:-2] + (1, shape[-1] // 4))) * (rng.random(shape[:-2] + (1, shape[-1] // 4)) > 0.0625), 4, axis=-1).astype(np.float32)
    return mx_ref.flush(v.astype(BF))
PG, PW = 8, 64
def bare(d):
    d["sm"][:, :, 4 * PG:] = 0; d["gs"][:, :, 8:] = 0
    return d
def sizes(rng, d):
    for n in ("sm", "gs"): d[n] = mx_ref.flush((d[n].astype(np.float32) * np.exp2(rng.integers(-12, 13, (N, 1, 1))).astype(np.float32)).astype(BF))
    return d
def setup_inputs(rng):
    return bare({"pg": f(rng, N, 128 * PG, 4 * PW), "sm": f(rng, N, 128, 512), "gs": f(rng, N, 128, 512), "qw": f(rng, N, 128, 1024)})
def setup_inputs_ties(rng):
    d = setup_inputs(rng); v = d["sm"].reshape(N, 128, 128, 4).copy()
    for q in range(N):
        k = rng.integers(PG // 4 + 1, PG // 2 + 1); p = rng.permutation(PG)
        v[q][:, p[k:]] = v[q][:, p[np.arange(k, PG) % k]]
    d["sm"] = v.reshape(N, 128, 512)
    d = sizes(rng, d)
    for r in rng.permutation(N)[:2]: d["gs"][r][:, 4:8] = 0
    return d
def setup_inputs_last(rng):
    d = setup_inputs(rng); c = f(rng, 128, 4)
    for r in range(N):
        j = rng.integers(0, 2)
        d["gs"][r][:, 4 * j:4 * j + 4] = c
        d["sm"][r][:, 4 * PG - 4:4 * PG] = (c.astype(np.float32) * 2).astype(BF)
    return d
def setup_inputs_alike(rng):
    d = setup_inputs(rng); d["gs"] = np.stack([d["gs"][0]] * N); return d
def setup_inputs_below(rng):
    d = setup_inputs(rng)
    d["gs"] = np.abs(d["gs"].astype(np.float32)).astype(BF)
    d["sm"] = (-np.abs(d["sm"].astype(np.float32))).astype(BF)
    return bare(sizes(rng, d))
def setup_inputs_spread(rng):
    d = setup_inputs(rng); d["pg"] = wide(rng, N, 128 * PG, 4 * PW); d["sm"] = wide(rng, N, 128, 512); d["gs"] = wide(rng, N, 128, 512)
    return bare(d)
def check_inputs(d):
    b = []
    for r in range(N):
        if d["sm"][r][:, 4 * PG:].astype(np.float32).any(): b.append("sm")
        if d["gs"][r][:, 8:].astype(np.float32).any(): b.append("gs")
    return b
def reference(pg, sm, gs, qw):
    S = [mx_ref.quantize(t) for t in sm]; G = [mx_ref.quantize(t) for t in gs]
    y = np.zeros((N, 128, 2 * N * PW), np.float32); ch = np.zeros((N, 2, N), np.float32)
    for r in range(N):
        W = [mx_ref.quantize(qw[r][:, 512 * j:512 * j + 512]) for j in range(2)]
        for q in range(N):
            score = mx_ref.matmul(S[q], G[r])
            for j in range(2):
                c = int(np.argmax(score[:PG, j]))
                k = PW * (j * N + q)
                y[r][:, k:k + PW] = mx_ref.matmul(W[j], mx_ref.quantize(pg[q][128 * c:128 * c + 128]))
                ch[r, j, q] = c
    return {"y": y, "ch": ch}

@@ -1,0 +1,358 @@
+from concourse.bass import DstId, RemoteDMATransfer
+from concourse.mybir import dt, AluOpType, ActivationFunctionType
+
+N, PG, PW = 8, 8, 64
+E = 4 * PW
+F8, U8, F32, BF, I32 = "float8_e4m3fn_x4", "uint8", "float32", "bfloat16", "int32"
+SCRATCH = {
+    "gsb": ("sbuf", [128, 512], BF), "smr": ("sbuf", [128, 512], BF),
+    "pgw": ("sbuf", [128, PG * E], BF), "qwb": ("sbuf", [128, 1024], BF),
+    "grc": ("sbuf", [128, 144], F8), "grp": ("sbuf", [128, 144], U8),
+    "smc": ("sbuf", [128, 192], F8), "smp": ("sbuf", [128, 192], U8),
+    "wc": ("sbuf", [128, 256], F8), "wp": ("sbuf", [128, 256], U8),
+    "h": ("sbuf", [128, 8 * 512], BF),
+    "qc": ("sbuf", [128, 7 * 128], F8), "qp": ("sbuf", [128, 7 * 128], U8),
+    "lc": ("sbuf", [128, N * 128], F8), "lp": ("sbuf", [128, N * 128], U8),
+    "rgc": ("sbuf", [128, 2], F8), "rgp": ("sbuf", [128, 8], U8),
+    "rsc": ("sbuf", [128, 8], F8), "rsp": ("sbuf", [128, 32], U8),
+    "rpc": ("sbuf", [128, 256], F8), "rpp": ("sbuf", [128, 256], U8),
+    "zz": ("sbuf", [128, 64], F32), "rb": ("sbuf", [128, 64], F32), "wt": ("sbuf", [128, 64], F32),
+    "ta": ("sbuf", [128, 16], I32), "tb": ("sbuf", [128, 16], I32), "tc": ("sbuf", [128, 16], I32),
+    "base": ("sbuf", [128, 16], F32),
+    "pc": ("sbuf", [128, 64], F32), "ic": ("sbuf", [128, 64], F32), "jc": ("sbuf", [128, 64], F32),
+    "kc": ("sbuf", [128, 64], F32), "chs": ("sbuf", [128, 8], F32),
+    "ysb": ("sbuf", [128, 1024], F32),
+}
+for _b in "DX":
+    SCRATCH["ts" + _b] = ("sbuf", [128, 32], F32)
+    SCRATCH["pm" + _b] = ("sbuf", [128, 8], F32)
+    SCRATCH["ind" + _b] = ("sbuf", [128, 64], F32)
+    SCRATCH["cc" + _b] = ("sbuf", [128, 64], F32)
+    SCRATCH["ct" + _b] = ("sbuf", [128, 32], F32)
+    SCRATCH["off" + _b] = ("sbuf", [128, 128], "uint16")
+for _i in range(8):
+    SCRATCH["ps%d" % _i] = ("psum", [128, 512], F32)
+SEMAPHORES = (["ldg", "lds", "ldp", "ldw", "v0", "vg", "v1", "vs", "v2", "v3", "it", "sgo", "gd", "gx", "sa",
+               "tD", "tX", "tC", "cD", "cX", "cC", "wq", "qda", "qdb", "qxa", "qxb", "qo",
+               "rg", "rs", "rc0", "rc1", "rp0", "rp1", "ls", "st", "sch"]
+              + ["%s%d" % (n, i) for n in ("fv", "fs", "hv", "hs", "pg", "ma", "mb", "yv", "ys") for i in range(8)])
+BIG = 1e29
+
+
+def relays(topo, rc, far):
+    c = [x for x in topo.cores_of(rc) if x != rc and all(topo.may_write(x, d) for d in far)]
+    near = [x for x in c if topo.die(x) == topo.die(rc)]
+    away = [x for x in c if topo.die(x) != topo.die(rc)]
+    return [near[0], away[0]]
+
+
+def classes(topo, cores, r):
+    same = [q for q in range(N) if q == r or topo.same_plane(cores[q], cores[r])]
+    return same, [q for q in range(N) if q not in same]
+
+
+def mask(es):
+    m = 0
+    for e in es:
+        m |= 1 << e
+    return m
+
+
+def rank_program(g, core, T, topo):
+    cores = T.cores
+    total, waited = {}, {}
+
+    def sem(n):
+        return T.sem[n]
+
+    def wait(eng, n, v):
+        eng.wait_ge(sem(n), v)
+        waited[n] = max(waited.get(n, 0), v)
+
+    def inc(inst, n, v=1):
+        inst.then_inc(sem(n), v)
+        total[n] = total.get(n, 0) + v
+
+    def fused(parts):
+        tr = []
+        for src, dsts, es, s in parts:
+            ids = []
+            for d, _ in dsts:
+                rid, pid = topo.addr(d, core)
+                ids.append(DstId(rid=rid, pnc=pid))
+            tr.append(RemoteDMATransfer(dst_ids=ids, dma_engine_mask=mask(es), remote_sem=sem(s),
+                                        srcs=[src], dsts=[a for _, a in dsts]))
+            total["ls"] = total.get("ls", 0) + len(es)
+        g.remote_dma_fused(tr, local_sem=sem("ls"))
+
+    def send(src, d, dst, es, s):
+        rid, pid = topo.addr(d, core)
+        g.remote_dma(dst, src, sem(s), sem("ls"), pid, rid, mask(es))
+        total["ls"] = total.get("ls", 0) + len(es)
+
+    def cod(t, a, b):
+        return t[:, a:b].bitcast(dt.uint8)
+
+    def finish():
+        for n in total:
+            if waited.get(n, 0) < total[n]:
+                g.wait_ge(sem(n), total[n])
+
+    def sslot(q, d):
+        return 8 + 8 * (q if q < d else q - 1)
+
+    r = T.rank_of(core)
+    if r is None:
+        for q in range(N):
+            if core in topo.cores_of(cores[q]):
+                same, other = classes(topo, cores, q)
+                rel = relays(topo, cores[q], [cores[d] for d in other])
+                if core in rel:
+                    relay_part(g, T, topo, core, cores, q, same.index(q), other, rel.index(core), wait, fused, send, cod, sslot)
+                    finish()
+        return
+
+    same, other = classes(topo, cores, r)
+    n4 = len(same)
+    s = same.index(r)
+    rel = relays(topo, core, [cores[d] for d in other])
+    dD = [same[(s + 1 + k) % n4] for k in range(n4 - 1)]
+    off = topo.engines(core, cores[dD[0]])
+    far = [e for e in topo.engines(core, rel[0]) if e not in off]
+    hf = len(off) // 2
+    V, S, TE = g.vector, g.scalar, g.tensor
+    ADD, MAX, MIN, MUL = AluOpType.add, AluOpType.max, AluOpType.min, AluOpType.mult
+    LT, GT = AluOpType.is_lt, AluOpType.is_gt
+    CP = ActivationFunctionType.Copy
+
+    inc(g.sync.dma_start(T.gsb[:, 0:8], T.gs[:, 0:8]), "ldg", 16)
+    inc(S.dma_start(T.smr[:, 0:128], T.sm[:, 0:128]), "lds", 16)
+    for m in range(PG):
+        e = g.sync if m % 2 == 0 else S
+        if m == PG // 2 or m == PG // 2 + 1:
+            wait(e, "sgo", 1)
+        inc(e.dma_start(T.pgw[:, E * m:E * m + E], T.pg[128 * m:128 * m + 128, :]), "ldp", 16)
+    inc(g.sync.dma_start(T.qwb[:], T.qw[:]), "ldw", 16)
+
+    inc(g.iota(T.ta[:], [[0, 16]], 0, 1), "it")
+    inc(g.iota(T.tb[:], [[16, 16]], 0, 0), "it")
+    inc(g.iota(T.wt[:], [[0, 8], [1, 8]], 0, 0, allow_small_or_imprecise_dtypes=True), "it")
+
+    wait(g, "vg", 1)
+    fused([(cod(T.grc, 16, 18), [(c, cod(T.rgc, 0, 2)) for c in rel], far[:hf], "rg"),
+           (T.grp[:, 16:24], [(c, T.rgp[:, 0:8]) for c in rel], far[hf:], "rg")])
+
+    def gslot(d):
+        return 10 + 2 * ((same.index(d) - s - 1) % n4)
+    fused([(cod(T.grc, 16, 18), [(cores[d], cod(T.grc, gslot(d), gslot(d) + 2)) for d in dD], off[:hf], "gd")])
+    fused([(T.grp[:, 16:18], [(cores[d], T.grp[:, gslot(d):gslot(d) + 2]) for d in dD], off[hf:], "gd")])
+    g.sem_inc(sem("sgo"), 1)
+    wait(g, "vs", 1)
+    fused([(cod(T.smc, 64, 72), [(c, cod(T.rsc, 0, 8)) for c in rel], far[:hf], "rs"),
+           (T.smp[:, 64:96], [(c, T.rsp[:, 0:32]) for c in rel], far[hf:], "rs")])
+    fused([(cod(T.smc, 64, 72), [(cores[d], cod(T.smc, sslot(r, d), sslot(r, d) + 8)) for d in dD], off[:hf], "sa")])
+    fused([(T.smp[:, 64:72], [(cores[d], T.smp[:, sslot(r, d):sslot(r, d) + 8]) for d in dD], off[hf:], "sa")])
+
+    def cq(k):
+        return cod(T.qc, 128 * k, 128 * k + 128)
+
+    def pq(k):
+        return T.qp[:, 128 * k:128 * k + 128]
+    lcd, lpd = cod(T.lc, 128 * r, 128 * r + 128), T.lp[:, 128 * r:128 * r + 128]
+    pn = "pg%d" % r
+    wait(g, "qda", 2)
+    fused([(cq(k), [(cores[dD[k]], lcd)], off[hf * k:hf * k + hf], pn) for k in range(2)])
+    fused([(pq(k), [(cores[dD[k]], lpd)], off[hf * k:hf * k + hf], pn) for k in range(2)])
+    wait(g, "qdb", 1)
+    send(cq(2), cores[dD[2]], lcd, off, pn)
+    send(pq(2), cores[dD[2]], lpd, off, pn)
+    for t in range(2):
+        wait(g, ("qxa", "qxb")[t], 2)
+        fused([(cq(3 + 2 * t + a), [(rel[a], cod(T.rpc, 128 * t, 128 * t + 128))], (off, far)[a], "rc%d" % t) for a in range(2)])
+        fused([(pq(3 + 2 * t + a), [(rel[a], T.rpp[:, 128 * t:128 * t + 128])], (off, far)[a], "rp%d" % t) for a in range(2)])
+
+    inc(V.memset(T.gsb[:, 8:512], 0.0), "v0")
+    for t in ("zz", "indD", "indX"):
+        inc(V.memset(T[t][:], 0.0), "v2")
+    wait(V, "v0", 1)
+    wait(V, "ldg", 16)
+    inc(V.quantize_mx(T.grc[:, 16:144], T.grp[:, 16:144], T.gsb[:]), "vg")
+    wait(V, "lds", 16)
+    inc(V.tensor_copy(T.smr[:, 128:256], T.smr[:, 0:128]), "v1")
+    wait(V, "v1", 1)
+    inc(V.tensor_copy(T.smr[:, 256:512], T.smr[:, 0:256]), "v1")
+    wait(V, "v1", 2)
+    inc(V.quantize_mx(T.smc[:, 64:192], T.smp[:, 64:192], T.smr[:]), "vs")
+    inc(V.memset(T.rb[:], BIG), "v2")
+    inc(V.memset(T.ic[:], 0.0), "v2")
+    wait(V, "it", 3)
+    inc(V.tensor_scalar(T.tc[:], T.ta[:], 15, None, AluOpType.bitwise_and), "v2")
+    wait(V, "v2", 6)
+    inc(V.memset(T.rb[:, 0:64:8], -BIG), "v3")
+    inc(V.tensor_tensor(T.base[:], T.tc[:], T.tb[:], ADD), "v3")
+    wait(V, "v3", 2)
+
+    def chain(b, ps):
+        c = "c" + b
+        wait(V, "t" + b, 1)
+        inc(V.transpose(T["ts" + b][:], T[ps][:, 0:32]), c)
+        wait(V, c, 1)
+        inc(V.tensor_tensor_scan(T["pm" + b][:], T.zz[:, 0:8], T["ts" + b][:, 0:8], -BIG, ADD, MAX), c)
+        wait(V, c, 2)
+        inc(V.tensor_scalar(T["ind" + b][:, 24:32], T["pm" + b][:], T["pm" + b][:, 7:8], float(E), LT, MUL), c)
+        wait(V, c, 3)
+        inc(V.tensor_tensor_scan(T["cc" + b][:, 24:64], T["ind" + b][:, 24:64], T.zz[:, 0:40], 0.0, ADD, ADD), c)
+        wait(V, c, 4)
+        inc(V.transpose(T["ct" + b][:], T["cc" + b][:, 32:64]), c)
+        wait(V, c, 5)
+
+    def offs(b, i, n):
+        inc(V.tensor_scalar(T["off" + b][:, 16 * i:16 * i + 16], T.base[:], T["ct" + b][:, i:i + 1], None, ADD), n)
+
+    def gather(eng, b, i, d, j, n):
+        out = T.h[:, 512 * d + E * j:512 * d + E * j + E]
+        win = T.pgw[:, 0:PG * E].indirect(T["off" + b][:, 16 * i:16 * i + 16])
+        if eng == "V":
+            inc(V.tensor_copy(out, win), n)
+        else:
+            inc(S.activation(out, win, CP), n)
+
+    def quant(d, n):
+        o = (T.lc[:, 128 * r:128 * r + 128], T.lp[:, 128 * r:128 * r + 128]) if d == 7 else \
+            (T.qc[:, 128 * d:128 * d + 128], T.qp[:, 128 * d:128 * d + 128])
+        inc(V.quantize_mx(o[0], o[1], T.h[:, 512 * d:512 * d + 512]), n)
+
+    chain("D", "ps0")
+    cold = [2 * ((s - same.index(d) - 1) % n4) for d in dD]
+    wait(V, "ldp", 16 * PG)
+    wait(S, "ldp", 16 * PG)
+    for k in range(3):
+        offs("D", cold[k] + 1, "fs%d" % k)
+        offs("D", cold[k], "fv%d" % k)
+        wait(V, "fv%d" % k, 1)
+        gather("V", "D", cold[k], k, 0, "hv%d" % k)
+        wait(S, "fs%d" % k, 1)
+        gather("S", "D", cold[k] + 1, k, 1, "hs%d" % k)
+        wait(V, "hv%d" % k, 1)
+        wait(V, "hs%d" % k, 1)
+        quant(k, "qda" if k < 2 else "qdb")
+
+    chain("X", "ps1")
+    colx = [2 * ((s + k) % n4) for k in range(4)]
+    for t in range(2):
+        for k in (2 * t, 2 * t + 1):
+            offs("X", colx[k] + 1, "fs%d" % (3 + k))
+            offs("X", colx[k], "fv%d" % (3 + k) if k < 3 else "fs%d" % (3 + k))
+        if t == 0:
+            for k in (0, 1):
+                wait(V, "fv%d" % (3 + k), 1)
+                gather("V", "X", colx[k], 3 + k, 0, "hv%d" % (3 + k))
+    for k in range(4):
+        wait(S, "fs%d" % (3 + k), 1 if k < 3 else 2)
+        gather("S", "X", colx[k] + 1, 3 + k, 1, "hs%d" % (3 + k))
+        if k == 3:
+            gather("S", "X", colx[k], 3 + k, 0, "hs%d" % (3 + k))
+    for k in (0, 1):
+        wait(V, "hv%d" % (3 + k), 1)
+        wait(V, "hs%d" % (3 + k), 1)
+        quant(3 + k, "qxa")
+    wait(V, "fv5", 1)
+    gather("V", "X", colx[2], 5, 0, "hv5")
+    wait(V, "hv5", 1)
+    wait(V, "hs5", 1)
+    quant(5, "qxb")
+    wait(V, "hs6", 2)
+    quant(6, "qxb")
+
+    offs("D", 7, "fs7")
+    offs("D", 6, "fv7")
+    wait(V, "fv7", 1)
+    gather("V", "D", 6, 7, 0, "hv7")
+    wait(S, "fs7", 1)
+    gather("S", "D", 7, 7, 1, "hs7")
+    wait(V, "ldw", 16)
+    inc(V.quantize_mx(T.wc[:], T.wp[:], T.qwb[:]), "wq")
+    wait(V, "hv7", 1)
+    wait(V, "hs7", 1)
+    quant(7, "qo")
+    wait(V, "tC", 1)
+    inc(V.tensor_tensor_scan(T.pc[0:2, :], T.rb[0:2, :], T.ps2[0:2, 0:64], 0.0, MIN, MAX), "cC")
+    wait(V, "cC", 1)
+    inc(V.tensor_tensor(T.ic[0:2, 1:64], T.pc[0:2, 1:64], T.pc[0:2, 0:63], GT), "cC")
+    wait(V, "cC", 2)
+    inc(V.tensor_tensor(T.jc[0:2, :], T.ic[0:2, :], T.wt[0:2, :], MUL), "cC")
+    wait(V, "cC", 3)
+    inc(V.tensor_tensor_scan(T.kc[0:2, :], T.rb[0:2, :], T.jc[0:2, :], 0.0, MIN, MAX), "cC")
+    wait(V, "cC", 4)
+    if r > 0:
+        inc(V.tensor_copy(T.chs[0:2, 0:r], T.kc[0:2, 7:8 * r:8]), "sch")
+    if r < N - 1:
+        inc(V.tensor_copy(T.chs[0:2, r + 1:N], T.kc[0:2, 8 * r + 7:56:8]), "sch")
+    inc(V.tensor_copy(T.chs[0:2, r:r + 1], T.kc[0:2, 63:64]), "sch")
+
+    own = (T.smc[:, 64:192], T.smp[:, 64:192])
+    wait(TE, "vg", 1)
+    wait(TE, "vs", 1)
+    wait(TE, "gd", 2 * hf * (n4 - 1))
+    inc(TE.matmul_mx(T.ps0[:, 0:128], own[0], own[1], T.grc[:, 10:138], T.grp[:, 10:138], True, True), "tD")
+    wait(TE, "gx", 2 * hf * n4)
+    inc(TE.matmul_mx(T.ps1[:, 0:128], own[0], own[1], T.grc[:, 2:130], T.grp[:, 2:130], True, True), "tX")
+    wait(TE, "sa", 2 * hf * (N - 1))
+    inc(TE.matmul_mx(T.ps2[:, 0:128], T.grc[:, 16:144], T.grp[:, 16:144], T.smc[:, 8:136], T.smp[:, 8:136], True, True), "tC")
+    order = [r] + [same[(s - 1 - k) % n4] for k in range(3)] + [other[(s - k) % n4] for k in range(4)]
+    banks = [(3, 4), (5, 6), (7, 0), (1, 2)]
+    wait(TE, "wq", 1)
+    wait(g.sync, "sch", total["sch"])
+    inc(g.sync.dma_start(T.ch[:], T.chs[0:2, :]), "st", 16)
+    for n in range(N):
+        q = order[n]
+        if n == 0:
+            wait(TE, "qo", 1)
+        else:
+            wait(TE, "pg%d" % q, 2 * hf if n < 3 else 4 * hf)
+        if n == 2:
+            wait(TE, "cD", 5)
+        if n == 3:
+            wait(TE, "cX", 5)
+            wait(TE, "cC", 4)
+        if n >= 4:
+            wait(TE, "yv%d" % (n - 4), 1)
+            wait(TE, "ys%d" % (n - 4), 1)
+        for j in range(2):
+            inc(TE.matmul_mx(T["ps%d" % banks[n % 4][j]][:, 0:128], T.wc[:, 128 * j:128 * j + 128], T.wp[:, 128 * j:128 * j + 128],
+                             T.lc[:, 128 * q:128 * q + 128], T.lp[:, 128 * q:128 * q + 128], True, True), "%s%d" % (("ma", "mb")[j], n))
+        a, b = PW * q, PW * (N + q)
+        wait(V, "ma%d" % n, 1)
+        inc(V.tensor_copy(T.ysb[:, a:a + PW], T["ps%d" % banks[n % 4][0]][:, 0:PW]), "yv%d" % n)
+        wait(S, "mb%d" % n, 1)
+        inc(S.activation(T.ysb[:, b:b + PW], T["ps%d" % banks[n % 4][1]][:, PW:2 * PW], CP), "ys%d" % n)
+        wait(g.sync, "yv%d" % n, 1)
+        inc(g.sync.dma_start(T.y[:, a:a + PW], T.ysb[:, a:a + PW]), "st", 16)
+        if n < N - 2:
+            wait(g.sync, "ys%d" % n, 1)
+            inc(g.sync.dma_start(T.y[:, b:b + PW], T.ysb[:, b:b + PW]), "st", 16)
+    for n in (N - 2, N - 1):
+        b = PW * (N + order[n])
+        wait(S, "ys%d" % n, 1)
+        inc(S.dma_start(T.y[:, b:b + PW], T.ysb[:, b:b + PW]), "st", 16)
+    finish()
+
+
+def relay_part(g, T, topo, core, cores, q, s, other, a, wait, fused, send, cod, sslot):
+    n4 = len(other)
+    dst = [other[(s + a + 2 * t) % n4] for t in range(2)]
+    es = topo.engines(core, cores[dst[0]])
+    hf = len(es) // 2
+    wait(g, "rg", 2 * hf)
+    k = 2 + 2 * s
+    fused([(cod(T.rgc, 0, 2), [(cores[d], cod(T.grc, k, k + 2)) for d in dst], es[:hf], "gx")])
+    fused([(T.rgp[:, 0:2], [(cores[d], T.grp[:, k:k + 2]) for d in dst], es[hf:], "gx")])
+    wait(g, "rs", 2 * hf)
+    fused([(cod(T.rsc, 0, 8), [(cores[d], cod(T.smc, sslot(q, d), sslot(q, d) + 8)) for d in dst], es[:hf], "sa")])
+    fused([(T.rsp[:, 0:8], [(cores[d], T.smp[:, sslot(q, d):sslot(q, d) + 8]) for d in dst], es[hf:], "sa")])
+    for t in range(2):
+        c0, c1 = 128 * t, 128 * t + 128
+        wait(g, "rc%d" % t, len(es))
+        send(cod(T.rpc, c0, c1), cores[dst[t]], cod(T.lc, 128 * q, 128 * q + 128), es, "pg%d" % q)
+        wait(g, "rp%d" % t, len(es))
+        send(T.rpp[:, c0:c1], cores[dst[t]], T.lp[:, 128 * q:128 * q + 128], es, "pg%d" % q)

@@ -32,9 +32,9 @@ for _b in "DX":
     SCRATCH["off" + _b] = ("sbuf", [128, 128], "uint16")
 for _i in range(8):
     SCRATCH["ps%d" % _i] = ("psum", [128, 512], F32)
-SEMAPHORES = (["ldg", "lds", "ldp", "ldw", "v0", "vg", "v1", "vs", "v2", "v3", "it", "sgo", "gd", "gx", "sa",
+SEMAPHORES = (["ldg", "lds", "ldp", "ldw", "v0", "vg", "v1", "vs", "v2", "v3", "it", "lg", "gd", "gx", "sa",
                "tD", "tX", "tC", "cD", "cX", "cC", "wq", "qda", "qdb", "qxa", "qxb", "qo",
-               "rg", "rs", "rc0", "rc1", "rp0", "rp1", "ls", "st", "sch"]
+               "rg", "rs", "rp0", "rp1", "ls", "st", "sch"]
               + ["%s%d" % (n, i) for n in ("fv", "fs", "hv", "hs", "pg", "ma", "mb", "yv", "ys") for i in range(8)])
 BIG = 1e29
 
@@ -43,7 +43,7 @@ def relays(topo, rc, far):
     c = [x for x in topo.cores_of(rc) if x != rc and all(topo.may_write(x, d) for d in far)]
     near = [x for x in c if topo.die(x) == topo.die(rc)]
     away = [x for x in c if topo.die(x) != topo.die(rc)]
-    return [near[0], away[0]]
+    return [near[0], away[0]], [near[1], away[1]]
 
 
 def classes(topo, cores, r):
@@ -73,7 +73,7 @@ def rank_program(g, core, T, topo):
         inst.then_inc(sem(n), v)
         total[n] = total.get(n, 0) + v
 
-    def fused(parts):
+    def fused(parts, ls="ls"):
         tr = []
         for src, dsts, es, s in parts:
             ids = []
@@ -82,8 +82,8 @@ def rank_program(g, core, T, topo):
                 ids.append(DstId(rid=rid, pnc=pid))
             tr.append(RemoteDMATransfer(dst_ids=ids, dma_engine_mask=mask(es), remote_sem=sem(s),
                                         srcs=[src], dsts=[a for _, a in dsts]))
-            total["ls"] = total.get("ls", 0) + len(es)
-        g.remote_dma_fused(tr, local_sem=sem("ls"))
+            total[ls] = total.get(ls, 0) + len(es)
+        g.remote_dma_fused(tr, local_sem=sem(ls))
 
     def send(src, d, dst, es, s):
         rid, pid = topo.addr(d, core)
@@ -106,19 +106,20 @@ def rank_program(g, core, T, topo):
         for q in range(N):
             if core in topo.cores_of(cores[q]):
                 same, other = classes(topo, cores, q)
-                rel = relays(topo, cores[q], [cores[d] for d in other])
-                if core in rel:
-                    relay_part(g, T, topo, core, cores, q, same.index(q), other, rel.index(core), wait, fused, send, cod, sslot)
-                    finish()
+                for b, rel in enumerate(relays(topo, cores[q], [cores[d] for d in other])):
+                    if core in rel:
+                        relay_part(g, T, topo, core, cores, q, same.index(q), other, rel.index(core), b, wait, fused, send, cod,
+                                   sslot)
+                        finish()
         return
 
     same, other = classes(topo, cores, r)
     n4 = len(same)
     s = same.index(r)
-    rel = relays(topo, core, [cores[d] for d in other])
+    relc, relp = relays(topo, core, [cores[d] for d in other])
     dD = [same[(s + 1 + k) % n4] for k in range(n4 - 1)]
     off = topo.engines(core, cores[dD[0]])
-    far = [e for e in topo.engines(core, rel[0]) if e not in off]
+    far = [e for e in topo.engines(core, relc[0]) if e not in off]
     hf = len(off) // 2
     V, S, TE = g.vector, g.scalar, g.tensor
     ADD, MAX, MIN, MUL = AluOpType.add, AluOpType.max, AluOpType.min, AluOpType.mult
@@ -129,9 +130,8 @@ def rank_program(g, core, T, topo):
     inc(S.dma_start(T.smr[:, 0:128], T.sm[:, 0:128]), "lds", 16)
     for m in range(PG):
         e = g.sync if m % 2 == 0 else S
-        if m == PG // 2 or m == PG // 2 + 1:
-            wait(e, "sgo", 1)
         inc(e.dma_start(T.pgw[:, E * m:E * m + E], T.pg[128 * m:128 * m + 128, :]), "ldp", 16)
+    wait(g.sync, "lg", 2 * hf)
     inc(g.sync.dma_start(T.qwb[:], T.qw[:]), "ldw", 16)
 
     inc(g.iota(T.ta[:], [[0, 16]], 0, 1), "it")
@@ -139,17 +139,16 @@ def rank_program(g, core, T, topo):
     inc(g.iota(T.wt[:], [[0, 8], [1, 8]], 0, 0, allow_small_or_imprecise_dtypes=True), "it")
 
     wait(g, "vg", 1)
-    fused([(cod(T.grc, 16, 18), [(c, cod(T.rgc, 0, 2)) for c in rel], far[:hf], "rg"),
-           (T.grp[:, 16:24], [(c, T.rgp[:, 0:8]) for c in rel], far[hf:], "rg")])
+    fused([(cod(T.grc, 16, 18), [(c, cod(T.rgc, 0, 2)) for c in relc], far[:hf], "rg"),
+           (T.grp[:, 16:24], [(c, T.rgp[:, 0:8]) for c in relp], far[hf:], "rg")], "lg")
 
     def gslot(d):
         return 10 + 2 * ((same.index(d) - s - 1) % n4)
     fused([(cod(T.grc, 16, 18), [(cores[d], cod(T.grc, gslot(d), gslot(d) + 2)) for d in dD], off[:hf], "gd")])
     fused([(T.grp[:, 16:18], [(cores[d], T.grp[:, gslot(d):gslot(d) + 2]) for d in dD], off[hf:], "gd")])
-    g.sem_inc(sem("sgo"), 1)
     wait(g, "vs", 1)
-    fused([(cod(T.smc, 64, 72), [(c, cod(T.rsc, 0, 8)) for c in rel], far[:hf], "rs"),
-           (T.smp[:, 64:96], [(c, T.rsp[:, 0:32]) for c in rel], far[hf:], "rs")])
+    fused([(cod(T.smc, 64, 72), [(c, cod(T.rsc, 0, 8)) for c in relc], far[:hf], "rs"),
+           (T.smp[:, 64:96], [(c, T.rsp[:, 0:32]) for c in relp], far[hf:], "rs")])
     fused([(cod(T.smc, 64, 72), [(cores[d], cod(T.smc, sslot(r, d), sslot(r, d) + 8)) for d in dD], off[:hf], "sa")])
     fused([(T.smp[:, 64:72], [(cores[d], T.smp[:, sslot(r, d):sslot(r, d) + 8]) for d in dD], off[hf:], "sa")])
 
@@ -163,13 +162,13 @@ def rank_program(g, core, T, topo):
     wait(g, "qda", 2)
     fused([(cq(k), [(cores[dD[k]], lcd)], off[hf * k:hf * k + hf], pn) for k in range(2)])
     fused([(pq(k), [(cores[dD[k]], lpd)], off[hf * k:hf * k + hf], pn) for k in range(2)])
+    for t in range(2):
+        wait(g, ("qxa", "qxb")[t], 2)
+        fused([(cq(3 + 2 * t + a), [(relc[a], cod(T.rpc, 128 * t, 128 * t + 128))], (off, far)[a], "rp%d" % t) for a in range(2)])
+        fused([(pq(3 + 2 * t + a), [(relp[a], T.rpp[:, 128 * t:128 * t + 128])], (off, far)[a], "rp%d" % t) for a in range(2)])
     wait(g, "qdb", 1)
     send(cq(2), cores[dD[2]], lcd, off, pn)
     send(pq(2), cores[dD[2]], lpd, off, pn)
-    for t in range(2):
-        wait(g, ("qxa", "qxb")[t], 2)
-        fused([(cq(3 + 2 * t + a), [(rel[a], cod(T.rpc, 128 * t, 128 * t + 128))], (off, far)[a], "rc%d" % t) for a in range(2)])
-        fused([(pq(3 + 2 * t + a), [(rel[a], T.rpp[:, 128 * t:128 * t + 128])], (off, far)[a], "rp%d" % t) for a in range(2)])
 
     inc(V.memset(T.gsb[:, 8:512], 0.0), "v0")
     for t in ("zz", "indD", "indX"):
@@ -209,150 +208,160 @@ def rank_program(g, core, T, topo):
     def offs(b, i, n):
         inc(V.tensor_scalar(T["off" + b][:, 16 * i:16 * i + 16], T.base[:], T["ct" + b][:, i:i + 1], None, ADD), n)
 
-    def gather(eng, b, i, d, j, n):
-        out = T.h[:, 512 * d + E * j:512 * d + E * j + E]
-        win = T.pgw[:, 0:PG * E].indirect(T["off" + b][:, 16 * i:16 * i + 16])
+    def lists(b, i, d, eng):
+        for j in range(2):
+            offs(b, i + j, "f%s%d" % (eng, d))
+
+    def gather(eng, b, i, d, j, w):
+        out = T.h[:, 512 * d + E * j:512 * d + E * (j + w)]
+        win = T.pgw[:, 0:PG * E].indirect(T["off" + b][:, 16 * i:16 * (i + w)])
         if eng == "V":
-            inc(V.tensor_copy(out, win), n)
+            wait(V, "fv%d" % d, w)
+            inc(V.tensor_copy(out, win), "hv%d" % d)
         else:
-            inc(S.activation(out, win, CP), n)
+            wait(S, "fs%d" % d, w)
+            inc(S.activation(out, win, CP), "hs%d" % d)
 
     def quant(d, n):
         o = (T.lc[:, 128 * r:128 * r + 128], T.lp[:, 128 * r:128 * r + 128]) if d == 7 else \
             (T.qc[:, 128 * d:128 * d + 128], T.qp[:, 128 * d:128 * d + 128])
         inc(V.quantize_mx(o[0], o[1], T.h[:, 512 * d:512 * d + 512]), n)
 
+    def pair(b, iv, dv, i2, d2, n):
+        gather("S", b, i2, d2, 0, 2)
+        gather("V", b, iv, dv, 0, 2)
+        wait(V, "hv%d" % dv, 1)
+        quant(dv, n)
+        wait(V, "hs%d" % d2, 1)
+        quant(d2, n)
+
+    def halves(b, i, d):
+        offs(b, i + 1, "fs%d" % d)
+        offs(b, i, "fv%d" % d)
+        gather("S", b, i + 1, d, 1, 1)
+        gather("V", b, i, d, 0, 1)
+
+    def done(d, n):
+        wait(V, "hv%d" % d, 1)
+        wait(V, "hs%d" % d, 1)
+        quant(d, n)
+
+    pe, ot = [same[(s - 1 - k) % n4] for k in range(n4 - 1)], [other[(s - k) % n4] for k in range(n4)]
+    order = pe[:2] + [r] + ot[:2] + pe[2:] + ot[2:]
+    banks = [(3, 4), (5, 6), (7, 0), (1, 2)]
+
+    def out(n):
+        a, b = PW * order[n], PW * (N + order[n])
+        pa, pb = (T["ps%d" % k] for k in banks[n % 4])
+        wait(S, "mb%d" % n, 1)
+        inc(S.activation(T.ysb[:, b:b + PW], pb[:, PW:2 * PW], CP), "ys%d" % n)
+        if n < 2:
+            wait(S, "ma%d" % n, 1)
+            inc(S.activation(T.ysb[:, a:a + PW], pa[:, 0:PW], CP), "yv%d" % n)
+        else:
+            wait(V, "ma%d" % n, 1)
+            inc(V.tensor_copy(T.ysb[:, a:a + PW], pa[:, 0:PW]), "yv%d" % n)
+
     chain("D", "ps0")
     cold = [2 * ((s - same.index(d) - 1) % n4) for d in dD]
+    lists("D", cold[1], 1, "s")
+    lists("D", cold[0], 0, "v")
     wait(V, "ldp", 16 * PG)
     wait(S, "ldp", 16 * PG)
-    for k in range(3):
-        offs("D", cold[k] + 1, "fs%d" % k)
-        offs("D", cold[k], "fv%d" % k)
-        wait(V, "fv%d" % k, 1)
-        gather("V", "D", cold[k], k, 0, "hv%d" % k)
-        wait(S, "fs%d" % k, 1)
-        gather("S", "D", cold[k] + 1, k, 1, "hs%d" % k)
-        wait(V, "hv%d" % k, 1)
-        wait(V, "hs%d" % k, 1)
-        quant(k, "qda" if k < 2 else "qdb")
+    pair("D", cold[0], 0, cold[1], 1, "qda")
 
     chain("X", "ps1")
     colx = [2 * ((s + k) % n4) for k in range(4)]
-    for t in range(2):
-        for k in (2 * t, 2 * t + 1):
-            offs("X", colx[k] + 1, "fs%d" % (3 + k))
-            offs("X", colx[k], "fv%d" % (3 + k) if k < 3 else "fs%d" % (3 + k))
-        if t == 0:
-            for k in (0, 1):
-                wait(V, "fv%d" % (3 + k), 1)
-                gather("V", "X", colx[k], 3 + k, 0, "hv%d" % (3 + k))
-    for k in range(4):
-        wait(S, "fs%d" % (3 + k), 1 if k < 3 else 2)
-        gather("S", "X", colx[k] + 1, 3 + k, 1, "hs%d" % (3 + k))
-        if k == 3:
-            gather("S", "X", colx[k], 3 + k, 0, "hs%d" % (3 + k))
-    for k in (0, 1):
-        wait(V, "hv%d" % (3 + k), 1)
-        wait(V, "hs%d" % (3 + k), 1)
-        quant(3 + k, "qxa")
-    wait(V, "fv5", 1)
-    gather("V", "X", colx[2], 5, 0, "hv5")
-    wait(V, "hv5", 1)
-    wait(V, "hs5", 1)
-    quant(5, "qxb")
-    wait(V, "hs6", 2)
+    lists("X", colx[1], 4, "s")
+    lists("X", colx[0], 3, "v")
+    lists("X", colx[3], 6, "s")
+    pair("X", colx[0], 3, colx[1], 4, "qxa")
+    gather("S", "X", colx[3], 6, 0, 2)
+    halves("X", colx[2], 5)
+    wait(V, "hs6", 1)
     quant(6, "qxb")
-
-    offs("D", 7, "fs7")
-    offs("D", 6, "fv7")
-    wait(V, "fv7", 1)
-    gather("V", "D", 6, 7, 0, "hv7")
-    wait(S, "fs7", 1)
-    gather("S", "D", 7, 7, 1, "hs7")
+    done(5, "qxb")
     wait(V, "ldw", 16)
     inc(V.quantize_mx(T.wc[:], T.wp[:], T.qwb[:]), "wq")
-    wait(V, "hv7", 1)
-    wait(V, "hs7", 1)
-    quant(7, "qo")
+    halves("D", cold[2], 2)
+    done(2, "qdb")
+
+    halves("D", 6, 7)
+    done(7, "qo")
     wait(V, "tC", 1)
     inc(V.tensor_tensor_scan(T.pc[0:2, :], T.rb[0:2, :], T.ps2[0:2, 0:64], 0.0, MIN, MAX), "cC")
-    wait(V, "cC", 1)
-    inc(V.tensor_tensor(T.ic[0:2, 1:64], T.pc[0:2, 1:64], T.pc[0:2, 0:63], GT), "cC")
-    wait(V, "cC", 2)
-    inc(V.tensor_tensor(T.jc[0:2, :], T.ic[0:2, :], T.wt[0:2, :], MUL), "cC")
-    wait(V, "cC", 3)
-    inc(V.tensor_tensor_scan(T.kc[0:2, :], T.rb[0:2, :], T.jc[0:2, :], 0.0, MIN, MAX), "cC")
-    wait(V, "cC", 4)
-    if r > 0:
-        inc(V.tensor_copy(T.chs[0:2, 0:r], T.kc[0:2, 7:8 * r:8]), "sch")
-    if r < N - 1:
-        inc(V.tensor_copy(T.chs[0:2, r + 1:N], T.kc[0:2, 8 * r + 7:56:8]), "sch")
-    inc(V.tensor_copy(T.chs[0:2, r:r + 1], T.kc[0:2, 63:64]), "sch")
+
+    def choices():
+        wait(V, "cC", 1)
+        inc(V.tensor_tensor(T.ic[0:2, 1:64], T.pc[0:2, 1:64], T.pc[0:2, 0:63], GT), "cC")
+        wait(V, "cC", 2)
+        inc(V.tensor_tensor(T.jc[0:2, :], T.ic[0:2, :], T.wt[0:2, :], MUL), "cC")
+        wait(V, "cC", 3)
+        inc(V.tensor_tensor_scan(T.kc[0:2, :], T.rb[0:2, :], T.jc[0:2, :], 0.0, MIN, MAX), "cC")
+        wait(V, "cC", 4)
+        if r > 0:
+            inc(V.tensor_copy(T.chs[0:2, 0:r], T.kc[0:2, 7:8 * r:8]), "sch")
+        if r < N - 1:
+            inc(V.tensor_copy(T.chs[0:2, r + 1:N], T.kc[0:2, 8 * r + 7:56:8]), "sch")
+        inc(V.tensor_copy(T.chs[0:2, r:r + 1], T.kc[0:2, 63:64]), "sch")
 
     own = (T.smc[:, 64:192], T.smp[:, 64:192])
     wait(TE, "vg", 1)
     wait(TE, "vs", 1)
     wait(TE, "gd", 2 * hf * (n4 - 1))
     inc(TE.matmul_mx(T.ps0[:, 0:128], own[0], own[1], T.grc[:, 10:138], T.grp[:, 10:138], True, True), "tD")
-    wait(TE, "gx", 2 * hf * n4)
+    wait(TE, "gx", 4 * hf * n4)
     inc(TE.matmul_mx(T.ps1[:, 0:128], own[0], own[1], T.grc[:, 2:130], T.grp[:, 2:130], True, True), "tX")
-    wait(TE, "sa", 2 * hf * (N - 1))
+    wait(TE, "sa", 2 * hf * (n4 - 1) + 4 * hf * n4)
     inc(TE.matmul_mx(T.ps2[:, 0:128], T.grc[:, 16:144], T.grp[:, 16:144], T.smc[:, 8:136], T.smp[:, 8:136], True, True), "tC")
-    order = [r] + [same[(s - 1 - k) % n4] for k in range(3)] + [other[(s - k) % n4] for k in range(4)]
-    banks = [(3, 4), (5, 6), (7, 0), (1, 2)]
     wait(TE, "wq", 1)
-    wait(g.sync, "sch", total["sch"])
-    inc(g.sync.dma_start(T.ch[:], T.chs[0:2, :]), "st", 16)
+    held = order.index(pe[2])
     for n in range(N):
         q = order[n]
-        if n == 0:
+        if q == r:
             wait(TE, "qo", 1)
         else:
-            wait(TE, "pg%d" % q, 2 * hf if n < 3 else 4 * hf)
+            wait(TE, "pg%d" % q, 2 * hf if q in pe[:2] else 4 * hf)
         if n == 2:
             wait(TE, "cD", 5)
         if n == 3:
             wait(TE, "cX", 5)
-            wait(TE, "cC", 4)
+            wait(TE, "cC", 1)
         if n >= 4:
             wait(TE, "yv%d" % (n - 4), 1)
             wait(TE, "ys%d" % (n - 4), 1)
-        for j in range(2):
+        for j in (1, 0):
             inc(TE.matmul_mx(T["ps%d" % banks[n % 4][j]][:, 0:128], T.wc[:, 128 * j:128 * j + 128], T.wp[:, 128 * j:128 * j + 128],
                              T.lc[:, 128 * q:128 * q + 128], T.lp[:, 128 * q:128 * q + 128], True, True), "%s%d" % (("ma", "mb")[j], n))
-        a, b = PW * q, PW * (N + q)
-        wait(V, "ma%d" % n, 1)
-        inc(V.tensor_copy(T.ysb[:, a:a + PW], T["ps%d" % banks[n % 4][0]][:, 0:PW]), "yv%d" % n)
-        wait(S, "mb%d" % n, 1)
-        inc(S.activation(T.ysb[:, b:b + PW], T["ps%d" % banks[n % 4][1]][:, PW:2 * PW], CP), "ys%d" % n)
-        wait(g.sync, "yv%d" % n, 1)
-        inc(g.sync.dma_start(T.y[:, a:a + PW], T.ysb[:, a:a + PW]), "st", 16)
-        if n < N - 2:
-            wait(g.sync, "ys%d" % n, 1)
-            inc(g.sync.dma_start(T.y[:, b:b + PW], T.ysb[:, b:b + PW]), "st", 16)
-    for n in (N - 2, N - 1):
-        b = PW * (N + order[n])
-        wait(S, "ys%d" % n, 1)
-        inc(S.dma_start(T.y[:, b:b + PW], T.ysb[:, b:b + PW]), "st", 16)
+        out(n)
+        if n == 4:
+            choices()
+        if n != held:
+            ms = [held, n] if n == N - 1 else [n]
+            lo = PW * min(order[m] for m in ms)
+            for e, nm, a in ((S if n == N - 1 else g.sync, "ys", PW * N + lo), (g.sync, "yv", lo)):
+                for m in ms:
+                    wait(e, "%s%d" % (nm, m), 1)
+                b = a + PW * len(ms)
+                inc(e.dma_start(T.y[:, a:b], T.ysb[:, a:b]), "st", 16)
+        if n == 4:
+            wait(g.sync, "sch", total["sch"])
+            inc(g.sync.dma_start(T.ch[:], T.chs[0:2, :]), "st", 16)
     finish()
 
 
-def relay_part(g, T, topo, core, cores, q, s, other, a, wait, fused, send, cod, sslot):
+def relay_part(g, T, topo, core, cores, q, s, other, a, b, wait, fused, send, cod, sslot):
     n4 = len(other)
     dst = [other[(s + a + 2 * t) % n4] for t in range(2)]
     es = topo.engines(core, cores[dst[0]])
-    hf = len(es) // 2
-    wait(g, "rg", 2 * hf)
+
+    def v(c, p, i, j):
+        return T[p][:, i:j] if b else cod(T[c], i, j)
+    wait(g, "rg", len(es) // 2)
     k = 2 + 2 * s
-    fused([(cod(T.rgc, 0, 2), [(cores[d], cod(T.grc, k, k + 2)) for d in dst], es[:hf], "gx")])
-    fused([(T.rgp[:, 0:2], [(cores[d], T.grp[:, k:k + 2]) for d in dst], es[hf:], "gx")])
-    wait(g, "rs", 2 * hf)
-    fused([(cod(T.rsc, 0, 8), [(cores[d], cod(T.smc, sslot(q, d), sslot(q, d) + 8)) for d in dst], es[:hf], "sa")])
-    fused([(T.rsp[:, 0:8], [(cores[d], T.smp[:, sslot(q, d):sslot(q, d) + 8]) for d in dst], es[hf:], "sa")])
+    fused([(v("rgc", "rgp", 0, 2), [(cores[d], v("grc", "grp", k, k + 2)) for d in dst], es, "gx")])
+    wait(g, "rs", len(es) // 2)
+    fused([(v("rsc", "rsp", 0, 8), [(cores[d], v("smc", "smp", sslot(q, d), sslot(q, d) + 8)) for d in dst], es, "sa")])
     for t in range(2):
-        c0, c1 = 128 * t, 128 * t + 128
-        wait(g, "rc%d" % t, len(es))
-        send(cod(T.rpc, c0, c1), cores[dst[t]], cod(T.lc, 128 * q, 128 * q + 128), es, "pg%d" % q)
         wait(g, "rp%d" % t, len(es))
-        send(T.rpp[:, c0:c1], cores[dst[t]], T.lp[:, 128 * q:128 * q + 128], es, "pg%d" % q)
+        send(v("rpc", "rpp", 128 * t, 128 * t + 128), cores[dst[t]], v("lc", "lp", 128 * q, 128 * q + 128), es, "pg%d" % q)

from concourse.bass import DstId, RemoteDMATransfer
from concourse.mybir import dt, AluOpType, ActivationFunctionType

N, PG, PW = 8, 8, 64
E = 4 * PW
F8, U8, F32, BF, I32 = "float8_e4m3fn_x4", "uint8", "float32", "bfloat16", "int32"
SCRATCH = {
    "gsb": ("sbuf", [128, 512], BF), "smr": ("sbuf", [128, 512], BF),
    "pgw": ("sbuf", [128, PG * E], BF), "qwb": ("sbuf", [128, 1024], BF),
    "grc": ("sbuf", [128, 144], F8), "grp": ("sbuf", [128, 144], U8),
    "smc": ("sbuf", [128, 192], F8), "smp": ("sbuf", [128, 192], U8),
    "wc": ("sbuf", [128, 256], F8), "wp": ("sbuf", [128, 256], U8),
    "h": ("sbuf", [128, 8 * 512], BF),
    "qc": ("sbuf", [128, 7 * 128], F8), "qp": ("sbuf", [128, 7 * 128], U8),
    "lc": ("sbuf", [128, N * 128], F8), "lp": ("sbuf", [128, N * 128], U8),
    "rgc": ("sbuf", [128, 2], F8), "rgp": ("sbuf", [128, 8], U8),
    "rsc": ("sbuf", [128, 8], F8), "rsp": ("sbuf", [128, 32], U8),
    "rpc": ("sbuf", [128, 256], F8), "rpp": ("sbuf", [128, 256], U8),
    "zz": ("sbuf", [128, 64], F32), "rb": ("sbuf", [128, 64], F32), "wt": ("sbuf", [128, 64], F32),
    "ta": ("sbuf", [128, 16], I32), "tb": ("sbuf", [128, 16], I32), "tc": ("sbuf", [128, 16], I32),
    "base": ("sbuf", [128, 16], F32),
    "pc": ("sbuf", [128, 64], F32), "ic": ("sbuf", [128, 64], F32), "jc": ("sbuf", [128, 64], F32),
    "kc": ("sbuf", [128, 64], F32), "chs": ("sbuf", [128, 8], F32),
    "ysb": ("sbuf", [128, 1024], F32),
}
for _b in "DX":
    SCRATCH["ts" + _b] = ("sbuf", [128, 32], F32)
    SCRATCH["pm" + _b] = ("sbuf", [128, 8], F32)
    SCRATCH["ind" + _b] = ("sbuf", [128, 64], F32)
    SCRATCH["cc" + _b] = ("sbuf", [128, 64], F32)
    SCRATCH["ct" + _b] = ("sbuf", [128, 32], F32)
    SCRATCH["off" + _b] = ("sbuf", [128, 128], "uint16")
for _i in range(8):
    SCRATCH["ps%d" % _i] = ("psum", [128, 512], F32)
SEMAPHORES = (["ldg", "lds", "ldp", "ldw", "v0", "vg", "v1", "vs", "v2", "v3", "it", "lg", "gd", "gx", "sa",
               "tD", "tX", "tC", "cD", "cX", "cC", "wq", "qda", "qdb", "qxa", "qxb", "qo",
               "rg", "rs", "rp0", "rp1", "ls", "st", "sch"]
              + ["%s%d" % (n, i) for n in ("fv", "fs", "hv", "hs", "pg", "ma", "mb", "yv", "ys") for i in range(8)])
BIG = 1e29


def relays(topo, rc, far):
    c = [x for x in topo.cores_of(rc) if x != rc and all(topo.may_write(x, d) for d in far)]
    near = [x for x in c if topo.die(x) == topo.die(rc)]
    away = [x for x in c if topo.die(x) != topo.die(rc)]
    return [near[0], away[0]], [near[1], away[1]]


def classes(topo, cores, r):
    same = [q for q in range(N) if q == r or topo.same_plane(cores[q], cores[r])]
    return same, [q for q in range(N) if q not in same]


def mask(es):
    m = 0
    for e in es:
        m |= 1 << e
    return m


def rank_program(g, core, T, topo):
    cores = T.cores
    total, waited = {}, {}

    def sem(n):
        return T.sem[n]

    def wait(eng, n, v):
        eng.wait_ge(sem(n), v)
        waited[n] = max(waited.get(n, 0), v)

    def inc(inst, n, v=1):
        inst.then_inc(sem(n), v)
        total[n] = total.get(n, 0) + v

    def fused(parts, ls="ls"):
        tr = []
        for src, dsts, es, s in parts:
            ids = []
            for d, _ in dsts:
                rid, pid = topo.addr(d, core)
                ids.append(DstId(rid=rid, pnc=pid))
            tr.append(RemoteDMATransfer(dst_ids=ids, dma_engine_mask=mask(es), remote_sem=sem(s),
                                        srcs=[src], dsts=[a for _, a in dsts]))
            total[ls] = total.get(ls, 0) + len(es)
        g.remote_dma_fused(tr, local_sem=sem(ls))

    def send(src, d, dst, es, s):
        rid, pid = topo.addr(d, core)
        g.remote_dma(dst, src, sem(s), sem("ls"), pid, rid, mask(es))
        total["ls"] = total.get("ls", 0) + len(es)

    def cod(t, a, b):
        return t[:, a:b].bitcast(dt.uint8)

    def finish():
        for n in total:
            if waited.get(n, 0) < total[n]:
                g.wait_ge(sem(n), total[n])

    def sslot(q, d):
        return 8 + 8 * (q if q < d else q - 1)

    r = T.rank_of(core)
    if r is None:
        for q in range(N):
            if core in topo.cores_of(cores[q]):
                same, other = classes(topo, cores, q)
                for b, rel in enumerate(relays(topo, cores[q], [cores[d] for d in other])):
                    if core in rel:
                        relay_part(g, T, topo, core, cores, q, same.index(q), other, rel.index(core), b, wait, fused, send, cod,
                                   sslot)
                        finish()
        return

    same, other = classes(topo, cores, r)
    n4 = len(same)
    s = same.index(r)
    relc, relp = relays(topo, core, [cores[d] for d in other])
    dD = [same[(s + 1 + k) % n4] for k in range(n4 - 1)]
    off = topo.engines(core, cores[dD[0]])
    far = [e for e in topo.engines(core, relc[0]) if e not in off]
    hf = len(off) // 2
    V, S, TE = g.vector, g.scalar, g.tensor
    ADD, MAX, MIN, MUL = AluOpType.add, AluOpType.max, AluOpType.min, AluOpType.mult
    LT, GT = AluOpType.is_lt, AluOpType.is_gt
    CP = ActivationFunctionType.Copy

    inc(g.sync.dma_start(T.gsb[:, 0:8], T.gs[:, 0:8]), "ldg", 16)
    inc(S.dma_start(T.smr[:, 0:128], T.sm[:, 0:128]), "lds", 16)
    for m in range(PG):
        e = g.sync if m % 2 == 0 else S
        inc(e.dma_start(T.pgw[:, E * m:E * m + E], T.pg[128 * m:128 * m + 128, :]), "ldp", 16)
    wait(g.sync, "lg", 2 * hf)
    inc(g.sync.dma_start(T.qwb[:], T.qw[:]), "ldw", 16)

    inc(g.iota(T.ta[:], [[0, 16]], 0, 1), "it")
    inc(g.iota(T.tb[:], [[16, 16]], 0, 0), "it")
    inc(g.iota(T.wt[:], [[0, 8], [1, 8]], 0, 0, allow_small_or_imprecise_dtypes=True), "it")

    wait(g, "vg", 1)
    fused([(cod(T.grc, 16, 18), [(c, cod(T.rgc, 0, 2)) for c in relc], far[:hf], "rg"),
           (T.grp[:, 16:24], [(c, T.rgp[:, 0:8]) for c in relp], far[hf:], "rg")], "lg")

    def gslot(d):
        return 10 + 2 * ((same.index(d) - s - 1) % n4)
    fused([(cod(T.grc, 16, 18), [(cores[d], cod(T.grc, gslot(d), gslot(d) + 2)) for d in dD], off[:hf], "gd")])
    fused([(T.grp[:, 16:18], [(cores[d], T.grp[:, gslot(d):gslot(d) + 2]) for d in dD], off[hf:], "gd")])
    wait(g, "vs", 1)
    fused([(cod(T.smc, 64, 72), [(c, cod(T.rsc, 0, 8)) for c in relc], far[:hf], "rs"),
           (T.smp[:, 64:96], [(c, T.rsp[:, 0:32]) for c in relp], far[hf:], "rs")])
    fused([(cod(T.smc, 64, 72), [(cores[d], cod(T.smc, sslot(r, d), sslot(r, d) + 8)) for d in dD], off[:hf], "sa")])
    fused([(T.smp[:, 64:72], [(cores[d], T.smp[:, sslot(r, d):sslot(r, d) + 8]) for d in dD], off[hf:], "sa")])

    def cq(k):
        return cod(T.qc, 128 * k, 128 * k + 128)

    def pq(k):
        return T.qp[:, 128 * k:128 * k + 128]
    lcd, lpd = cod(T.lc, 128 * r, 128 * r + 128), T.lp[:, 128 * r:128 * r + 128]
    pn = "pg%d" % r
    wait(g, "qda", 2)
    fused([(cq(k), [(cores[dD[k]], lcd)], off[hf * k:hf * k + hf], pn) for k in range(2)])
    fused([(pq(k), [(cores[dD[k]], lpd)], off[hf * k:hf * k + hf], pn) for k in range(2)])
    for t in range(2):
        wait(g, ("qxa", "qxb")[t], 2)
        fused([(cq(3 + 2 * t + a), [(relc[a], cod(T.rpc, 128 * t, 128 * t + 128))], (off, far)[a], "rp%d" % t) for a in range(2)])
        fused([(pq(3 + 2 * t + a), [(relp[a], T.rpp[:, 128 * t:128 * t + 128])], (off, far)[a], "rp%d" % t) for a in range(2)])
    wait(g, "qdb", 1)
    send(cq(2), cores[dD[2]], lcd, off, pn)
    send(pq(2), cores[dD[2]], lpd, off, pn)

    inc(V.memset(T.gsb[:, 8:512], 0.0), "v0")
    for t in ("zz", "indD", "indX"):
        inc(V.memset(T[t][:], 0.0), "v2")
    wait(V, "v0", 1)
    wait(V, "ldg", 16)
    inc(V.quantize_mx(T.grc[:, 16:144], T.grp[:, 16:144], T.gsb[:]), "vg")
    wait(V, "lds", 16)
    inc(V.tensor_copy(T.smr[:, 128:256], T.smr[:, 0:128]), "v1")
    wait(V, "v1", 1)
    inc(V.tensor_copy(T.smr[:, 256:512], T.smr[:, 0:256]), "v1")
    wait(V, "v1", 2)
    inc(V.quantize_mx(T.smc[:, 64:192], T.smp[:, 64:192], T.smr[:]), "vs")
    inc(V.memset(T.rb[:], BIG), "v2")
    inc(V.memset(T.ic[:], 0.0), "v2")
    wait(V, "it", 3)
    inc(V.tensor_scalar(T.tc[:], T.ta[:], 15, None, AluOpType.bitwise_and), "v2")
    wait(V, "v2", 6)
    inc(V.memset(T.rb[:, 0:64:8], -BIG), "v3")
    inc(V.tensor_tensor(T.base[:], T.tc[:], T.tb[:], ADD), "v3")
    wait(V, "v3", 2)

    def chain(b, ps):
        c = "c" + b
        wait(V, "t" + b, 1)
        inc(V.transpose(T["ts" + b][:], T[ps][:, 0:32]), c)
        wait(V, c, 1)
        inc(V.tensor_tensor_scan(T["pm" + b][:], T.zz[:, 0:8], T["ts" + b][:, 0:8], -BIG, ADD, MAX), c)
        wait(V, c, 2)
        inc(V.tensor_scalar(T["ind" + b][:, 24:32], T["pm" + b][:], T["pm" + b][:, 7:8], float(E), LT, MUL), c)
        wait(V, c, 3)
        inc(V.tensor_tensor_scan(T["cc" + b][:, 24:64], T["ind" + b][:, 24:64], T.zz[:, 0:40], 0.0, ADD, ADD), c)
        wait(V, c, 4)
        inc(V.transpose(T["ct" + b][:], T["cc" + b][:, 32:64]), c)
        wait(V, c, 5)

    def offs(b, i, n):
        inc(V.tensor_scalar(T["off" + b][:, 16 * i:16 * i + 16], T.base[:], T["ct" + b][:, i:i + 1], None, ADD), n)

    def lists(b, i, d, eng):
        for j in range(2):
            offs(b, i + j, "f%s%d" % (eng, d))

    def gather(eng, b, i, d, j, w):
        out = T.h[:, 512 * d + E * j:512 * d + E * (j + w)]
        win = T.pgw[:, 0:PG * E].indirect(T["off" + b][:, 16 * i:16 * (i + w)])
        if eng == "V":
            wait(V, "fv%d" % d, w)
            inc(V.tensor_copy(out, win), "hv%d" % d)
        else:
            wait(S, "fs%d" % d, w)
            inc(S.activation(out, win, CP), "hs%d" % d)

    def quant(d, n):
        o = (T.lc[:, 128 * r:128 * r + 128], T.lp[:, 128 * r:128 * r + 128]) if d == 7 else \
            (T.qc[:, 128 * d:128 * d + 128], T.qp[:, 128 * d:128 * d + 128])
        inc(V.quantize_mx(o[0], o[1], T.h[:, 512 * d:512 * d + 512]), n)

    def pair(b, iv, dv, i2, d2, n):
        gather("S", b, i2, d2, 0, 2)
        gather("V", b, iv, dv, 0, 2)
        wait(V, "hv%d" % dv, 1)
        quant(dv, n)
        wait(V, "hs%d" % d2, 1)
        quant(d2, n)

    def halves(b, i, d):
        offs(b, i + 1, "fs%d" % d)
        offs(b, i, "fv%d" % d)
        gather("S", b, i + 1, d, 1, 1)
        gather("V", b, i, d, 0, 1)

    def done(d, n):
        wait(V, "hv%d" % d, 1)
        wait(V, "hs%d" % d, 1)
        quant(d, n)

    pe, ot = [same[(s - 1 - k) % n4] for k in range(n4 - 1)], [other[(s - k) % n4] for k in range(n4)]
    order = pe[:2] + [r] + ot[:2] + pe[2:] + ot[2:]
    banks = [(3, 4), (5, 6), (7, 0), (1, 2)]

    def out(n):
        a, b = PW * order[n], PW * (N + order[n])
        pa, pb = (T["ps%d" % k] for k in banks[n % 4])
        wait(S, "mb%d" % n, 1)
        inc(S.activation(T.ysb[:, b:b + PW], pb[:, PW:2 * PW], CP), "ys%d" % n)
        if n < 2:
            wait(S, "ma%d" % n, 1)
            inc(S.activation(T.ysb[:, a:a + PW], pa[:, 0:PW], CP), "yv%d" % n)
        else:
            wait(V, "ma%d" % n, 1)
            inc(V.tensor_copy(T.ysb[:, a:a + PW], pa[:, 0:PW]), "yv%d" % n)

    chain("D", "ps0")
    cold = [2 * ((s - same.index(d) - 1) % n4) for d in dD]
    lists("D", cold[1], 1, "s")
    lists("D", cold[0], 0, "v")
    wait(V, "ldp", 16 * PG)
    wait(S, "ldp", 16 * PG)
    pair("D", cold[0], 0, cold[1], 1, "qda")

    chain("X", "ps1")
    colx = [2 * ((s + k) % n4) for k in range(4)]
    lists("X", colx[1], 4, "s")
    lists("X", colx[0], 3, "v")
    lists("X", colx[3], 6, "s")
    pair("X", colx[0], 3, colx[1], 4, "qxa")
    gather("S", "X", colx[3], 6, 0, 2)
    halves("X", colx[2], 5)
    wait(V, "hs6", 1)
    quant(6, "qxb")
    done(5, "qxb")
    wait(V, "ldw", 16)
    inc(V.quantize_mx(T.wc[:], T.wp[:], T.qwb[:]), "wq")
    halves("D", cold[2], 2)
    done(2, "qdb")

    halves("D", 6, 7)
    done(7, "qo")
    wait(V, "tC", 1)
    inc(V.tensor_tensor_scan(T.pc[0:2, :], T.rb[0:2, :], T.ps2[0:2, 0:64], 0.0, MIN, MAX), "cC")

    def choices():
        wait(V, "cC", 1)
        inc(V.tensor_tensor(T.ic[0:2, 1:64], T.pc[0:2, 1:64], T.pc[0:2, 0:63], GT), "cC")
        wait(V, "cC", 2)
        inc(V.tensor_tensor(T.jc[0:2, :], T.ic[0:2, :], T.wt[0:2, :], MUL), "cC")
        wait(V, "cC", 3)
        inc(V.tensor_tensor_scan(T.kc[0:2, :], T.rb[0:2, :], T.jc[0:2, :], 0.0, MIN, MAX), "cC")
        wait(V, "cC", 4)
        if r > 0:
            inc(V.tensor_copy(T.chs[0:2, 0:r], T.kc[0:2, 7:8 * r:8]), "sch")
        if r < N - 1:
            inc(V.tensor_copy(T.chs[0:2, r + 1:N], T.kc[0:2, 8 * r + 7:56:8]), "sch")
        inc(V.tensor_copy(T.chs[0:2, r:r + 1], T.kc[0:2, 63:64]), "sch")

    own = (T.smc[:, 64:192], T.smp[:, 64:192])
    wait(TE, "vg", 1)
    wait(TE, "vs", 1)
    wait(TE, "gd", 2 * hf * (n4 - 1))
    inc(TE.matmul_mx(T.ps0[:, 0:128], own[0], own[1], T.grc[:, 10:138], T.grp[:, 10:138], True, True), "tD")
    wait(TE, "gx", 4 * hf * n4)
    inc(TE.matmul_mx(T.ps1[:, 0:128], own[0], own[1], T.grc[:, 2:130], T.grp[:, 2:130], True, True), "tX")
    wait(TE, "sa", 2 * hf * (n4 - 1) + 4 * hf * n4)
    inc(TE.matmul_mx(T.ps2[:, 0:128], T.grc[:, 16:144], T.grp[:, 16:144], T.smc[:, 8:136], T.smp[:, 8:136], True, True), "tC")
    wait(TE, "wq", 1)
    held = order.index(pe[2])
    for n in range(N):
        q = order[n]
        if q == r:
            wait(TE, "qo", 1)
        else:
            wait(TE, "pg%d" % q, 2 * hf if q in pe[:2] else 4 * hf)
        if n == 2:
            wait(TE, "cD", 5)
        if n == 3:
            wait(TE, "cX", 5)
            wait(TE, "cC", 1)
        if n >= 4:
            wait(TE, "yv%d" % (n - 4), 1)
            wait(TE, "ys%d" % (n - 4), 1)
        for j in (1, 0):
            inc(TE.matmul_mx(T["ps%d" % banks[n % 4][j]][:, 0:128], T.wc[:, 128 * j:128 * j + 128], T.wp[:, 128 * j:128 * j + 128],
                             T.lc[:, 128 * q:128 * q + 128], T.lp[:, 128 * q:128 * q + 128], True, True), "%s%d" % (("ma", "mb")[j], n))
        out(n)
        if n == 4:
            choices()
        if n != held:
            ms = [held, n] if n == N - 1 else [n]
            lo = PW * min(order[m] for m in ms)
            for e, nm, a in ((S if n == N - 1 else g.sync, "ys", PW * N + lo), (g.sync, "yv", lo)):
                for m in ms:
                    wait(e, "%s%d" % (nm, m), 1)
                b = a + PW * len(ms)
                inc(e.dma_start(T.y[:, a:b], T.ysb[:, a:b]), "st", 16)
        if n == 4:
            wait(g.sync, "sch", total["sch"])
            inc(g.sync.dma_start(T.ch[:], T.chs[0:2, :]), "st", 16)
    finish()


def relay_part(g, T, topo, core, cores, q, s, other, a, b, wait, fused, send, cod, sslot):
    n4 = len(other)
    dst = [other[(s + a + 2 * t) % n4] for t in range(2)]
    es = topo.engines(core, cores[dst[0]])

    def v(c, p, i, j):
        return T[p][:, i:j] if b else cod(T[c], i, j)
    wait(g, "rg", len(es) // 2)
    k = 2 + 2 * s
    fused([(v("rgc", "rgp", 0, 2), [(cores[d], v("grc", "grp", k, k + 2)) for d in dst], es, "gx")])
    wait(g, "rs", len(es) // 2)
    fused([(v("rsc", "rsp", 0, 8), [(cores[d], v("smc", "smp", sslot(q, d), sslot(q, d) + 8)) for d in dst], es, "sa")])
    for t in range(2):
        wait(g, "rp%d" % t, len(es))
        send(v("rpc", "rpp", 128 * t, 128 * t + 128), cores[dst[t]], v("lc", "lp", 128 * q, 128 * q + 128), es, "pg%d" % q)
